import numpy as np
import ml_dtypes


def mxq(x, axis, fmt="e4m3"):
    dtype, down = {"e4m3": (ml_dtypes.float8_e4m3fn, 7), "e5m2": (ml_dtypes.float8_e5m2, 14)}[fmt]
    v = np.moveaxis(np.asarray(x, np.float32).astype(ml_dtypes.bfloat16).astype(np.float64), axis, -1)
    blocks = v.reshape(v.shape[:-1] + (-1, 32))
    amax = np.abs(blocks).max(-1, keepdims=True)
    byte = np.maximum(np.where(amax > 0, np.frexp(amax)[1] - 1 + 127, 0) - down, 1)
    scale = np.exp2(byte - 127.0)
    codes = (blocks / scale).astype(np.float32).astype(dtype).astype(np.float64)
    return np.moveaxis((codes * scale).reshape(v.shape), -1, axis)


WIDE = False


def mx_kscale(k):
    if not WIDE:
        return np.ones(k)
    levels = np.array([10, -10, 5, -5, 0])
    if k % 512:
        return np.exp2(np.random.permutation(np.resize(levels, k // 32))).repeat(32)
    a = np.empty((k // 512, 16))
    for p in range(k // 512):
        a[p, :8] = np.random.permutation(np.resize(levels, 8))
        for g in range(8):
            far = levels[np.abs(levels - a[p, g]) >= 10]
            a[p, g + 8] = far[np.random.randint(len(far))]
    return np.exp2(a.ravel()).repeat(32)


BF16 = ml_dtypes.bfloat16


def bf(x):
    return np.asarray(x, np.float32).astype(BF16)


def f64(x):
    return np.asarray(x).astype(np.float64)


D = 1024

RHO = 3.0
SPREAD = 0.3


def setup_inputs():
    d = mx_kscale(D)
    outgoing = np.exp(SPREAD * np.random.standard_normal(D))
    incoming = np.exp(SPREAD * np.random.standard_normal(D))
    w0 = np.random.standard_normal((D, D)) * outgoing[:, None] * incoming
    c = 1 + 0.1 * np.random.standard_normal((D, D))
    return {"w": bf(w0 * d[:, None] / d),
            "v": bf(RHO / D * c * w0)}


def reference(w, v):
    w = f64(w)
    a = np.eye(D) + f64(v) * w
    p = mxq(a, 1, "e4m3") @ mxq(a, 0, "e4m3")
    q = mxq(p, 1, "e4m3") @ mxq(p, 0, "e4m3")
    return q.T * w

@@ -1,0 +1,337 @@
+from contextlib import ExitStack
+
+import concourse.mybir as mybir
+from concourse.masks import make_identity
+
+D = 1024
+FLOPS = 2 * 2 * D * D * D
+
+F32 = mybir.dt.float32
+BF16 = mybir.dt.bfloat16
+U32 = mybir.dt.uint32
+U8 = mybir.dt.uint8
+FP8X4 = mybir.dt.float8_e4m3fn_x4
+MULT = mybir.AluOpType.mult
+ADD = mybir.AluOpType.add
+
+P = 128
+PACK = 4
+HALF = P * PACK
+QUAD = PACK * HALF
+RAW_PAD = 32
+VAL_PAD = 1024
+
+
+def tile_notears_acyclicity_gradient_s7_kernel(tc, w, v, out):
+    nc = tc.nc
+    with ExitStack() as ctx:
+        keep = ctx.enter_context(tc.tile_pool(name="keep", bufs=1))
+        work = ctx.enter_context(tc.tile_pool(name="work", bufs=4))
+        outs = ctx.enter_context(tc.tile_pool(name="outs", bufs=8))
+        psum = ctx.enter_context(tc.psum_pool(name="psum", bufs=8))
+        ctx.enter_context(tc.manual_schedule())
+
+        ident = keep.tile([P, P], F32, name="ident", align_bytes=64)
+        make_identity(nc, ident[:])
+
+        raw = {}
+        values, right_in, left_in, turned, sums = {}, {}, {}, {}, {}
+        right, left = {}, {}
+
+        def copy(engine, dst, src):
+            if engine == "S":
+                nc.scalar.copy(out=dst, in_=src)
+            else:
+                nc.vector.tensor_copy(out=dst, in_=src)
+
+        def quadrant(x, q):
+            g, h = q
+            return x[g * HALF : (g + 1) * HALF, h * HALF : (h + 1) * HALF].rearrange("(p t) j -> p t j", t=PACK)
+
+        def load(q):
+            for name, x in (("v", v), ("w", w)):
+                t = keep.tile([P, QUAD + RAW_PAD], BF16, name="%s%d%d" % (name, q[0], q[1]), align_bytes=64)
+                nc.sync.dma_start(out=t[:, 0:QUAD].rearrange("p (t j) -> p t j", t=PACK), in_=quadrant(x, q))
+                raw[name, q] = t
+
+        def product(q):
+            a = keep.tile([P, QUAD + VAL_PAD], BF16, name="a%d%d" % q, align_bytes=64)
+            values["A", q] = a
+            vq, wq = raw["v", q], raw["w", q]
+            nc.vector.tensor_tensor(
+                out=a[:, 0:QUAD].rearrange("p (u c e) -> p c u e", u=2, e=2),
+                in0=vq[:, 0:QUAD].rearrange("p (c u e) -> p c u e", u=2, e=2),
+                in1=wq[:, 0:QUAD].rearrange("p (c u e) -> p c u e", u=2, e=2),
+                op=MULT,
+            )
+            if q[0] == q[1]:
+                step = HALF + 1
+                exact = work.tile([P, PACK, P], F32, name="exact", align_bytes=64)
+                nc.vector.tensor_tensor(
+                    out=exact[:],
+                    in0=vq[:, 0 : PACK * step].rearrange("p (t x) -> p t x", t=PACK)[:, :, 0:HALF:PACK],
+                    in1=wq[:, 0 : PACK * step].rearrange("p (t x) -> p t x", t=PACK)[:, :, 0:HALF:PACK],
+                    op=MULT,
+                )
+                on_diagonal = (
+                    a[:, 0:3072]
+                    .rearrange("p (u x) -> p u x", u=2)[:, :, 0:514]
+                    .rearrange("p u (e y) -> p u e y", e=2)[:, :, :, 0:256:2]
+                )
+                nc.vector.tensor_tensor(
+                    out=on_diagonal,
+                    in0=exact[:].rearrange("p (u e) c -> p u e c", u=2),
+                    in1=ident[:].unsqueeze(1).unsqueeze(1).to_broadcast([P, 2, 2, P]),
+                    op=ADD,
+                )
+
+        def words_of(m, q, t, u):
+            start = (u * PACK + t if m == "A" else t * 2 + u) * 2 * P
+            return values[m, q][:, start : start + 2 * P].bitcast(F32)
+
+        def turn(m, q, half):
+            bank = psum.tile([P, HALF], F32, name="bank")
+            for i in range(2):
+                for u in range(2):
+                    at = (2 * i + u) * P
+                    nc.tensor.transpose(bank[:, at : at + P], words_of(m, q, 2 * half + i, u), ident[:])
+            turned[m, q, half] = bank
+
+        def gather_left(m, q, half, engine):
+            if (m, q) not in left_in:
+                left_in[m, q] = work.tile([P, QUAD], BF16, name="left_in", align_bytes=64)
+            words = left_in[m, q][:].bitcast(F32)
+            bank = turned[m, q, half]
+            if m == "A":
+                dst = words[:, half * HALF : (half + 1) * HALF].rearrange("p (i r u) -> p i r u", i=2, u=2)
+                src = bank[:].rearrange("p (i u r) -> p i r u", i=2, u=2)
+            else:
+                dst = words.rearrange("p (r h x) -> p r h x", h=2, x=PACK)[:, :, half, :]
+                src = bank[:].rearrange("p (x r) -> p r x", x=PACK)
+            copy(engine, dst, src)
+
+        def gather_right(m, q, half, engine):
+            if (m, q) not in right_in:
+                right_in[m, q] = work.tile([P, QUAD], BF16, name="right_in", align_bytes=64)
+            x, y = values[m, q], right_in[m, q]
+            if m == "A":
+                cols = slice(half * QUAD // 2, (half + 1) * QUAD // 2)
+                src = x[:, cols].rearrange("p (t c i) -> p c t i", t=PACK, i=PACK)
+                dst = y[:, cols].rearrange("p (c i t) -> p c t i", t=PACK, i=PACK)
+            else:
+                rows = slice(half * P // 2, (half + 1) * P // 2)
+                src = x[:].rearrange("p (t a r e) -> p a t r e", t=PACK, r=2, e=2)[:, rows]
+                dst = y[:].rearrange("p (e a r t) -> p a t r e", t=PACK, r=2, e=2)[:, rows]
+            copy(engine, dst, src)
+
+        def quantize(side, m, q):
+            source, target = (left_in, left) if side == "L" else (right_in, right)
+            codes = keep.tile([P, HALF], U32, name="codes%s%s%d%d" % (side, m, q[0], q[1]), align_bytes=64)
+            scales = keep.tile([P, HALF], U8, name="scales%s%s%d%d" % (side, m, q[0], q[1]), align_bytes=64)
+            nc.vector.quantize_mx(out=codes[:].bitcast(FP8X4), scales=scales[:], in_=source[m, q][:])
+            target[m, q] = (codes, scales)
+
+        def multiply(m, q, t, halves=(0, 1)):
+            g, c = q
+            if (m, q, t) not in sums:
+                bank = psum.tile([P, HALF], F32, name="bank")
+                sums[m, q, t] = [bank, 0]
+            bank = sums[m, q, t][0]
+            for h in halves:
+                if m == "P":
+                    fixed, moving, block = left["A", (g, h)], right["A", (h, c)], t
+                else:
+                    fixed, moving, block = right["P", (h, g)], left["P", (c, h)], 2 * (t % 2) + t // 2
+                cols = slice(block * P, (block + 1) * P)
+                done = sums[m, q, t][1]
+                nc.tensor.matmul_mx(
+                    out=bank[:],
+                    lhsT=fixed[0][:, cols].bitcast(FP8X4),
+                    lhsT_scale=fixed[1][:, cols],
+                    rhs=moving[0][:].bitcast(FP8X4),
+                    rhs_scale=moving[1][:],
+                    start=(done == 0),
+                    stop=(done == 1),
+                )
+                sums[m, q, t][1] = done + 1
+
+        def round_square(q, t, engine):
+            if ("P", q) not in values:
+                values["P", q] = work.tile([P, QUAD], BF16, name="square", align_bytes=64)
+            copy(engine, values["P", q][:, t * HALF : (t + 1) * HALF], sums["P", q, t][0][:])
+
+        def finish(q, t):
+            result = outs.tile([P, HALF], F32, name="result")
+            nc.vector.tensor_tensor(
+                out=result[:], in0=sums["Q", q, t][0][:], in1=raw["w", q][:, t * HALF : (t + 1) * HALF], op=MULT
+            )
+            nc.sync.dma_start(out=quadrant(out, q)[:, t, :], in_=result[:])
+
+        load((0, 0))
+        load((1, 1))
+        load((0, 1))
+        load((1, 0))
+        product((0, 0))
+        turn("A", (0, 0), 0)
+        turn("A", (0, 0), 1)
+        gather_right("A", (0, 0), 0, "S")
+        gather_right("A", (0, 0), 1, "S")
+        gather_left("A", (0, 0), 0, "S")
+        gather_left("A", (0, 0), 1, "S")
+        product((1, 1))
+        turn("A", (1, 1), 0)
+        turn("A", (1, 1), 1)
+        gather_right("A", (1, 1), 0, "S")
+        gather_right("A", (1, 1), 1, "S")
+        product((0, 1))
+        turn("A", (0, 1), 0)
+        turn("A", (0, 1), 1)
+        gather_right("A", (0, 1), 0, "V")
+        gather_left("A", (0, 1), 0, "S")
+        gather_left("A", (0, 1), 1, "S")
+        gather_left("A", (1, 1), 0, "S")
+        gather_left("A", (1, 1), 1, "S")
+        product((1, 0))
+        turn("A", (1, 0), 0)
+        turn("A", (1, 0), 1)
+        gather_right("A", (0, 1), 1, "V")
+        gather_left("A", (1, 0), 0, "S")
+        gather_left("A", (1, 0), 1, "S")
+        quantize("L", "A", (0, 0))
+        quantize("R", "A", (0, 1))
+        multiply("P", (0, 1), 0, (0,))
+        multiply("P", (0, 1), 1, (0,))
+        multiply("P", (0, 1), 2, (0,))
+        multiply("P", (0, 1), 3, (0,))
+        quantize("R", "A", (1, 1))
+        quantize("L", "A", (0, 1))
+        multiply("P", (0, 1), 0, (1,))
+        multiply("P", (0, 1), 1, (1,))
+        multiply("P", (0, 1), 2, (1,))
+        multiply("P", (0, 1), 3, (1,))
+        quantize("R", "A", (0, 0))
+        quantize("L", "A", (1, 1))
+        gather_right("A", (1, 0), 0, "V")
+        gather_right("A", (1, 0), 1, "S")
+        quantize("L", "A", (1, 0))
+        quantize("R", "A", (1, 0))
+        round_square((0, 1), 0, "S")
+        round_square((0, 1), 1, "S")
+        round_square((0, 1), 2, "V")
+        round_square((0, 1), 3, "V")
+        multiply("P", (0, 0), 0, (0,))
+        multiply("P", (0, 0), 0, (1,))
+        round_square((0, 0), 0, "S")
+        multiply("P", (0, 0), 1, (0,))
+        multiply("P", (0, 0), 1, (1,))
+        round_square((0, 0), 1, "S")
+        multiply("P", (0, 0), 2, (0,))
+        multiply("P", (0, 0), 2, (1,))
+        round_square((0, 0), 2, "S")
+        multiply("P", (0, 0), 3, (0,))
+        multiply("P", (0, 0), 3, (1,))
+        round_square((0, 0), 3, "S")
+        turn("P", (0, 1), 0)
+        turn("P", (0, 1), 1)
+        gather_right("P", (0, 1), 0, "V")
+        gather_right("P", (0, 1), 1, "V")
+        gather_left("P", (0, 1), 0, "S")
+        gather_left("P", (0, 1), 1, "S")
+        quantize("R", "P", (0, 1))
+        multiply("P", (1, 1), 0, (1,))
+        multiply("P", (1, 1), 0, (0,))
+        round_square((1, 1), 0, "S")
+        multiply("P", (1, 1), 1, (1,))
+        multiply("P", (1, 1), 1, (0,))
+        round_square((1, 1), 1, "S")
+        multiply("P", (1, 1), 2, (1,))
+        multiply("P", (1, 1), 2, (0,))
+        round_square((1, 1), 2, "S")
+        multiply("P", (1, 1), 3, (1,))
+        multiply("P", (1, 1), 3, (0,))
+        round_square((1, 1), 3, "S")
+        turn("P", (0, 0), 0)
+        turn("P", (0, 0), 1)
+        gather_right("P", (0, 0), 0, "V")
+        gather_right("P", (0, 0), 1, "V")
+        quantize("L", "P", (0, 1))
+        gather_left("P", (0, 0), 0, "S")
+        gather_left("P", (0, 0), 1, "S")
+        quantize("R", "P", (0, 0))
+        turn("P", (1, 1), 0)
+        turn("P", (1, 1), 1)
+        multiply("P", (1, 0), 0, (0,))
+        multiply("P", (1, 0), 0, (1,))
+        round_square((1, 0), 0, "S")
+        multiply("P", (1, 0), 1, (0,))
+        multiply("P", (1, 0), 1, (1,))
+        round_square((1, 0), 1, "S")
+        multiply("P", (1, 0), 2, (0,))
+        multiply("P", (1, 0), 2, (1,))
+        round_square((1, 0), 2, "S")
+        multiply("P", (1, 0), 3, (0,))
+        multiply("P", (1, 0), 3, (1,))
+        round_square((1, 0), 3, "S")
+        gather_right("P", (1, 1), 0, "V")
+        gather_right("P", (1, 1), 1, "V")
+        quantize("L", "P", (0, 0))
+        gather_left("P", (1, 1), 0, "S")
+        gather_left("P", (1, 1), 1, "S")
+        quantize("R", "P", (1, 1))
+        multiply("Q", (1, 0), 0, (0,))
+        multiply("Q", (1, 0), 0, (1,))
+        finish((1, 0), 0)
+        multiply("Q", (1, 0), 1, (0,))
+        multiply("Q", (1, 0), 1, (1,))
+        finish((1, 0), 1)
+        turn("P", (1, 0), 0)
+        turn("P", (1, 0), 1)
+        gather_right("P", (1, 0), 0, "V")
+        gather_right("P", (1, 0), 1, "V")
+        gather_left("P", (1, 0), 0, "S")
+        gather_left("P", (1, 0), 1, "S")
+        multiply("Q", (1, 0), 2, (0,))
+        multiply("Q", (1, 0), 2, (1,))
+        finish((1, 0), 2)
+        quantize("R", "P", (1, 0))
+        quantize("L", "P", (1, 1))
+        multiply("Q", (1, 0), 3, (0,))
+        multiply("Q", (1, 0), 3, (1,))
+        finish((1, 0), 3)
+        quantize("L", "P", (1, 0))
+        multiply("Q", (0, 0), 0, (0,))
+        multiply("Q", (0, 0), 0, (1,))
+        finish((0, 0), 0)
+        multiply("Q", (0, 0), 1, (0,))
+        multiply("Q", (0, 0), 1, (1,))
+        finish((0, 0), 1)
+        multiply("Q", (0, 0), 2, (0,))
+        multiply("Q", (0, 0), 2, (1,))
+        finish((0, 0), 2)
+        multiply("Q", (0, 0), 3, (0,))
+        multiply("Q", (0, 0), 3, (1,))
+        finish((0, 0), 3)
+        multiply("Q", (1, 1), 0, (1,))
+        multiply("Q", (1, 1), 0, (0,))
+        finish((1, 1), 0)
+        multiply("Q", (1, 1), 1, (1,))
+        multiply("Q", (1, 1), 1, (0,))
+        finish((1, 1), 1)
+        multiply("Q", (1, 1), 2, (1,))
+        multiply("Q", (1, 1), 2, (0,))
+        finish((1, 1), 2)
+        multiply("Q", (1, 1), 3, (1,))
+        multiply("Q", (1, 1), 3, (0,))
+        finish((1, 1), 3)
+        multiply("Q", (0, 1), 0, (0,))
+        multiply("Q", (0, 1), 0, (1,))
+        finish((0, 1), 0)
+        multiply("Q", (0, 1), 1, (0,))
+        multiply("Q", (0, 1), 1, (1,))
+        finish((0, 1), 1)
+        multiply("Q", (0, 1), 2, (0,))
+        multiply("Q", (0, 1), 2, (1,))
+        finish((0, 1), 2)
+        multiply("Q", (0, 1), 3, (0,))
+        multiply("Q", (0, 1), 3, (1,))
+        finish((0, 1), 3)

@@ -18,25 +18,45 @@ P = 128
 PACK = 4
 HALF = P * PACK
 QUAD = PACK * HALF
-RAW_PAD = 32
-VAL_PAD = 1024
+RUN = 2 * P
+PAD = 32
 
 
 def tile_notears_acyclicity_gradient_s7_kernel(tc, w, v, out):
     nc = tc.nc
     with ExitStack() as ctx:
         keep = ctx.enter_context(tc.tile_pool(name="keep", bufs=1))
-        work = ctx.enter_context(tc.tile_pool(name="work", bufs=4))
+        small = ctx.enter_context(tc.tile_pool(name="small", bufs=2))
         outs = ctx.enter_context(tc.tile_pool(name="outs", bufs=8))
-        psum = ctx.enter_context(tc.psum_pool(name="psum", bufs=8))
+        psum = ctx.enter_context(tc.psum_pool(name="psum", bufs=1))
         ctx.enter_context(tc.manual_schedule())
 
         ident = keep.tile([P, P], F32, name="ident", align_bytes=64)
         make_identity(nc, ident[:])
 
-        raw = {}
-        values, right_in, left_in, turned, sums = {}, {}, {}, {}, {}
-        right, left = {}, {}
+        def values(name, width):
+            return keep.tile([P, width], BF16, name=name, align_bytes=64)
+
+        quads = [(g, h) for g in range(2) for h in range(2)]
+        raw, exact, turned, sums, left, right = {}, {}, {}, {}, {}, {}
+        a_top = values("a_top", 2 * QUAD)
+        a_low = [values("a_low%d" % h, QUAD + PAD) for h in range(2)]
+        left_top = values("left_top", 2 * QUAD)
+        left_in = {("A", 0, h): left_top[:, h * QUAD : (h + 1) * QUAD] for h in range(2)}
+        for m, g, h in [("A", 1, 0), ("A", 1, 1)] + [("P", g, h) for g, h in quads]:
+            left_in[m, g, h] = values("left_in%s%d%d" % (m, g, h), QUAD)[:]
+        right_in = {(m, g, h): values("right_in%s%d%d" % (m, g, h), QUAD)[:] for m in "AP" for g, h in quads}
+        rounded = {q: values("rounded%d%d" % q, QUAD) for q in quads}
+        for side, planes in (("left", left), ("right", right)):
+            for m in "AP":
+                for g, h in quads:
+                    name = "%s%s%d%d" % (side, m, g, h)
+                    codes = keep.tile([P, HALF], U32, name="codes_" + name, align_bytes=64)
+                    scales = keep.tile([P, HALF], U8, name="scales_" + name, align_bytes=64)
+                    planes[m, g, h] = (codes, scales)
+
+        def bank_tile(b):
+            return psum.tile([P, HALF], F32, name="bank%d" % b, tag="bank%d" % b)
 
         def copy(engine, dst, src):
             if engine == "S":
@@ -44,294 +64,287 @@ def tile_notears_acyclicity_gradient_s7_kernel(tc, w, v, out):
             else:
                 nc.vector.tensor_copy(out=dst, in_=src)
 
-        def quadrant(x, q):
-            g, h = q
-            return x[g * HALF : (g + 1) * HALF, h * HALF : (h + 1) * HALF].rearrange("(p t) j -> p t j", t=PACK)
+        def rows(x, g):
+            return x[g * HALF : (g + 1) * HALF, :].rearrange("(p t) j -> p t j", t=PACK)
 
-        def load(q):
+        def load0(t):
             for name, x in (("v", v), ("w", w)):
-                t = keep.tile([P, QUAD + RAW_PAD], BF16, name="%s%d%d" % (name, q[0], q[1]), align_bytes=64)
-                nc.sync.dma_start(out=t[:, 0:QUAD].rearrange("p (t j) -> p t j", t=PACK), in_=quadrant(x, q))
-                raw[name, q] = t
+                raw[name, 0, t] = values("%s_top%d" % (name, t), D)
+                nc.sync.dma_start(out=raw[name, 0, t][:], in_=rows(x, 0)[:, t, :])
 
-        def product(q):
-            a = keep.tile([P, QUAD + VAL_PAD], BF16, name="a%d%d" % q, align_bytes=64)
-            values["A", q] = a
-            vq, wq = raw["v", q], raw["w", q]
+        def load1(h):
+            for name, x in (("v", v), ("w", w)):
+                raw[name, 1, h] = values("%s_low%d" % (name, h), QUAD + PAD)
+                nc.sync.dma_start(
+                    out=raw[name, 1, h][:, 0:QUAD].rearrange("p (t j) -> p t j", t=PACK),
+                    in_=rows(x, 1)[:, :, h * HALF : (h + 1) * HALF],
+                )
+
+        def product0(t):
             nc.vector.tensor_tensor(
-                out=a[:, 0:QUAD].rearrange("p (u c e) -> p c u e", u=2, e=2),
-                in0=vq[:, 0:QUAD].rearrange("p (c u e) -> p c u e", u=2, e=2),
-                in1=wq[:, 0:QUAD].rearrange("p (c u e) -> p c u e", u=2, e=2),
+                out=a_top[:, t * D : (t + 1) * D].rearrange("p (u x e) -> p u x e", u=2, e=2),
+                in0=raw["v", 0, t][:].rearrange("p (x u e) -> p u x e", u=2, e=2),
+                in1=raw["w", 0, t][:].rearrange("p (x u e) -> p u x e", u=2, e=2),
                 op=MULT,
             )
-            if q[0] == q[1]:
-                step = HALF + 1
-                exact = work.tile([P, PACK, P], F32, name="exact", align_bytes=64)
-                nc.vector.tensor_tensor(
-                    out=exact[:],
-                    in0=vq[:, 0 : PACK * step].rearrange("p (t x) -> p t x", t=PACK)[:, :, 0:HALF:PACK],
-                    in1=wq[:, 0 : PACK * step].rearrange("p (t x) -> p t x", t=PACK)[:, :, 0:HALF:PACK],
-                    op=MULT,
-                )
-                on_diagonal = (
-                    a[:, 0:3072]
-                    .rearrange("p (u x) -> p u x", u=2)[:, :, 0:514]
-                    .rearrange("p u (e y) -> p u e y", e=2)[:, :, :, 0:256:2]
-                )
-                nc.vector.tensor_tensor(
-                    out=on_diagonal,
-                    in0=exact[:].rearrange("p (u e) c -> p u e c", u=2),
-                    in1=ident[:].unsqueeze(1).unsqueeze(1).to_broadcast([P, 2, 2, P]),
-                    op=ADD,
-                )
 
-        def words_of(m, q, t, u):
-            start = (u * PACK + t if m == "A" else t * 2 + u) * 2 * P
-            return values[m, q][:, start : start + 2 * P].bitcast(F32)
-
-        def turn(m, q, half):
-            bank = psum.tile([P, HALF], F32, name="bank")
-            for i in range(2):
-                for u in range(2):
-                    at = (2 * i + u) * P
-                    nc.tensor.transpose(bank[:, at : at + P], words_of(m, q, 2 * half + i, u), ident[:])
-            turned[m, q, half] = bank
-
-        def gather_left(m, q, half, engine):
-            if (m, q) not in left_in:
-                left_in[m, q] = work.tile([P, QUAD], BF16, name="left_in", align_bytes=64)
-            words = left_in[m, q][:].bitcast(F32)
-            bank = turned[m, q, half]
-            if m == "A":
-                dst = words[:, half * HALF : (half + 1) * HALF].rearrange("p (i r u) -> p i r u", i=2, u=2)
-                src = bank[:].rearrange("p (i u r) -> p i r u", i=2, u=2)
-            else:
-                dst = words.rearrange("p (r h x) -> p r h x", h=2, x=PACK)[:, :, half, :]
-                src = bank[:].rearrange("p (x r) -> p r x", x=PACK)
-            copy(engine, dst, src)
-
-        def gather_right(m, q, half, engine):
-            if (m, q) not in right_in:
-                right_in[m, q] = work.tile([P, QUAD], BF16, name="right_in", align_bytes=64)
-            x, y = values[m, q], right_in[m, q]
-            if m == "A":
-                cols = slice(half * QUAD // 2, (half + 1) * QUAD // 2)
-                src = x[:, cols].rearrange("p (t c i) -> p c t i", t=PACK, i=PACK)
-                dst = y[:, cols].rearrange("p (c i t) -> p c t i", t=PACK, i=PACK)
-            else:
-                rows = slice(half * P // 2, (half + 1) * P // 2)
-                src = x[:].rearrange("p (t a r e) -> p a t r e", t=PACK, r=2, e=2)[:, rows]
-                dst = y[:].rearrange("p (e a r t) -> p a t r e", t=PACK, r=2, e=2)[:, rows]
-            copy(engine, dst, src)
-
-        def quantize(side, m, q):
-            source, target = (left_in, left) if side == "L" else (right_in, right)
-            codes = keep.tile([P, HALF], U32, name="codes%s%s%d%d" % (side, m, q[0], q[1]), align_bytes=64)
-            scales = keep.tile([P, HALF], U8, name="scales%s%s%d%d" % (side, m, q[0], q[1]), align_bytes=64)
-            nc.vector.quantize_mx(out=codes[:].bitcast(FP8X4), scales=scales[:], in_=source[m, q][:])
-            target[m, q] = (codes, scales)
-
-        def multiply(m, q, t, halves=(0, 1)):
-            g, c = q
-            if (m, q, t) not in sums:
-                bank = psum.tile([P, HALF], F32, name="bank")
-                sums[m, q, t] = [bank, 0]
-            bank = sums[m, q, t][0]
-            for h in halves:
-                if m == "P":
-                    fixed, moving, block = left["A", (g, h)], right["A", (h, c)], t
-                else:
-                    fixed, moving, block = right["P", (h, g)], left["P", (c, h)], 2 * (t % 2) + t // 2
-                cols = slice(block * P, (block + 1) * P)
-                done = sums[m, q, t][1]
-                nc.tensor.matmul_mx(
-                    out=bank[:],
-                    lhsT=fixed[0][:, cols].bitcast(FP8X4),
-                    lhsT_scale=fixed[1][:, cols],
-                    rhs=moving[0][:].bitcast(FP8X4),
-                    rhs_scale=moving[1][:],
-                    start=(done == 0),
-                    stop=(done == 1),
-                )
-                sums[m, q, t][1] = done + 1
-
-        def round_square(q, t, engine):
-            if ("P", q) not in values:
-                values["P", q] = work.tile([P, QUAD], BF16, name="square", align_bytes=64)
-            copy(engine, values["P", q][:, t * HALF : (t + 1) * HALF], sums["P", q, t][0][:])
-
-        def finish(q, t):
-            result = outs.tile([P, HALF], F32, name="result")
+        def product1(h, u):
             nc.vector.tensor_tensor(
-                out=result[:], in0=sums["Q", q, t][0][:], in1=raw["w", q][:, t * HALF : (t + 1) * HALF], op=MULT
+                out=a_low[h][:, u * D : (u + 1) * D].rearrange("p (x e) -> p x e", e=2),
+                in0=raw["v", 1, h][:, 0:QUAD].rearrange("p (x u e) -> p x u e", u=2, e=2)[:, :, u, :],
+                in1=raw["w", 1, h][:, 0:QUAD].rearrange("p (x u e) -> p x u e", u=2, e=2)[:, :, u, :],
+                op=MULT,
             )
-            nc.sync.dma_start(out=quadrant(out, q)[:, t, :], in_=result[:])
 
-        load((0, 0))
-        load((1, 1))
-        load((0, 1))
-        load((1, 0))
-        product((0, 0))
-        turn("A", (0, 0), 0)
-        turn("A", (0, 0), 1)
-        gather_right("A", (0, 0), 0, "S")
-        gather_right("A", (0, 0), 1, "S")
-        gather_left("A", (0, 0), 0, "S")
-        gather_left("A", (0, 0), 1, "S")
-        product((1, 1))
-        turn("A", (1, 1), 0)
-        turn("A", (1, 1), 1)
-        gather_right("A", (1, 1), 0, "S")
-        gather_right("A", (1, 1), 1, "S")
-        product((0, 1))
-        turn("A", (0, 1), 0)
-        turn("A", (0, 1), 1)
-        gather_right("A", (0, 1), 0, "V")
-        gather_left("A", (0, 1), 0, "S")
-        gather_left("A", (0, 1), 1, "S")
-        gather_left("A", (1, 1), 0, "S")
-        gather_left("A", (1, 1), 1, "S")
-        product((1, 0))
-        turn("A", (1, 0), 0)
-        turn("A", (1, 0), 1)
-        gather_right("A", (0, 1), 1, "V")
-        gather_left("A", (1, 0), 0, "S")
-        gather_left("A", (1, 0), 1, "S")
-        quantize("L", "A", (0, 0))
-        quantize("R", "A", (0, 1))
-        multiply("P", (0, 1), 0, (0,))
-        multiply("P", (0, 1), 1, (0,))
-        multiply("P", (0, 1), 2, (0,))
-        multiply("P", (0, 1), 3, (0,))
-        quantize("R", "A", (1, 1))
-        quantize("L", "A", (0, 1))
-        multiply("P", (0, 1), 0, (1,))
-        multiply("P", (0, 1), 1, (1,))
-        multiply("P", (0, 1), 2, (1,))
-        multiply("P", (0, 1), 3, (1,))
-        quantize("R", "A", (0, 0))
-        quantize("L", "A", (1, 1))
-        gather_right("A", (1, 0), 0, "V")
-        gather_right("A", (1, 0), 1, "S")
-        quantize("L", "A", (1, 0))
-        quantize("R", "A", (1, 0))
-        round_square((0, 1), 0, "S")
-        round_square((0, 1), 1, "S")
-        round_square((0, 1), 2, "V")
-        round_square((0, 1), 3, "V")
-        multiply("P", (0, 0), 0, (0,))
-        multiply("P", (0, 0), 0, (1,))
-        round_square((0, 0), 0, "S")
-        multiply("P", (0, 0), 1, (0,))
-        multiply("P", (0, 0), 1, (1,))
-        round_square((0, 0), 1, "S")
-        multiply("P", (0, 0), 2, (0,))
-        multiply("P", (0, 0), 2, (1,))
-        round_square((0, 0), 2, "S")
-        multiply("P", (0, 0), 3, (0,))
-        multiply("P", (0, 0), 3, (1,))
-        round_square((0, 0), 3, "S")
-        turn("P", (0, 1), 0)
-        turn("P", (0, 1), 1)
-        gather_right("P", (0, 1), 0, "V")
-        gather_right("P", (0, 1), 1, "V")
-        gather_left("P", (0, 1), 0, "S")
-        gather_left("P", (0, 1), 1, "S")
-        quantize("R", "P", (0, 1))
-        multiply("P", (1, 1), 0, (1,))
-        multiply("P", (1, 1), 0, (0,))
-        round_square((1, 1), 0, "S")
-        multiply("P", (1, 1), 1, (1,))
-        multiply("P", (1, 1), 1, (0,))
-        round_square((1, 1), 1, "S")
-        multiply("P", (1, 1), 2, (1,))
-        multiply("P", (1, 1), 2, (0,))
-        round_square((1, 1), 2, "S")
-        multiply("P", (1, 1), 3, (1,))
-        multiply("P", (1, 1), 3, (0,))
-        round_square((1, 1), 3, "S")
-        turn("P", (0, 0), 0)
-        turn("P", (0, 0), 1)
-        gather_right("P", (0, 0), 0, "V")
-        gather_right("P", (0, 0), 1, "V")
-        quantize("L", "P", (0, 1))
-        gather_left("P", (0, 0), 0, "S")
-        gather_left("P", (0, 0), 1, "S")
-        quantize("R", "P", (0, 0))
-        turn("P", (1, 1), 0)
-        turn("P", (1, 1), 1)
-        multiply("P", (1, 0), 0, (0,))
-        multiply("P", (1, 0), 0, (1,))
-        round_square((1, 0), 0, "S")
-        multiply("P", (1, 0), 1, (0,))
-        multiply("P", (1, 0), 1, (1,))
-        round_square((1, 0), 1, "S")
-        multiply("P", (1, 0), 2, (0,))
-        multiply("P", (1, 0), 2, (1,))
-        round_square((1, 0), 2, "S")
-        multiply("P", (1, 0), 3, (0,))
-        multiply("P", (1, 0), 3, (1,))
-        round_square((1, 0), 3, "S")
-        gather_right("P", (1, 1), 0, "V")
-        gather_right("P", (1, 1), 1, "V")
-        quantize("L", "P", (0, 0))
-        gather_left("P", (1, 1), 0, "S")
-        gather_left("P", (1, 1), 1, "S")
-        quantize("R", "P", (1, 1))
-        multiply("Q", (1, 0), 0, (0,))
-        multiply("Q", (1, 0), 0, (1,))
-        finish((1, 0), 0)
-        multiply("Q", (1, 0), 1, (0,))
-        multiply("Q", (1, 0), 1, (1,))
-        finish((1, 0), 1)
-        turn("P", (1, 0), 0)
-        turn("P", (1, 0), 1)
-        gather_right("P", (1, 0), 0, "V")
-        gather_right("P", (1, 0), 1, "V")
-        gather_left("P", (1, 0), 0, "S")
-        gather_left("P", (1, 0), 1, "S")
-        multiply("Q", (1, 0), 2, (0,))
-        multiply("Q", (1, 0), 2, (1,))
-        finish((1, 0), 2)
-        quantize("R", "P", (1, 0))
-        quantize("L", "P", (1, 1))
-        multiply("Q", (1, 0), 3, (0,))
-        multiply("Q", (1, 0), 3, (1,))
-        finish((1, 0), 3)
-        quantize("L", "P", (1, 0))
-        multiply("Q", (0, 0), 0, (0,))
-        multiply("Q", (0, 0), 0, (1,))
-        finish((0, 0), 0)
-        multiply("Q", (0, 0), 1, (0,))
-        multiply("Q", (0, 0), 1, (1,))
-        finish((0, 0), 1)
-        multiply("Q", (0, 0), 2, (0,))
-        multiply("Q", (0, 0), 2, (1,))
-        finish((0, 0), 2)
-        multiply("Q", (0, 0), 3, (0,))
-        multiply("Q", (0, 0), 3, (1,))
-        finish((0, 0), 3)
-        multiply("Q", (1, 1), 0, (1,))
-        multiply("Q", (1, 1), 0, (0,))
-        finish((1, 1), 0)
-        multiply("Q", (1, 1), 1, (1,))
-        multiply("Q", (1, 1), 1, (0,))
-        finish((1, 1), 1)
-        multiply("Q", (1, 1), 2, (1,))
-        multiply("Q", (1, 1), 2, (0,))
-        finish((1, 1), 2)
-        multiply("Q", (1, 1), 3, (1,))
-        multiply("Q", (1, 1), 3, (0,))
-        finish((1, 1), 3)
-        multiply("Q", (0, 1), 0, (0,))
-        multiply("Q", (0, 1), 0, (1,))
-        finish((0, 1), 0)
-        multiply("Q", (0, 1), 1, (0,))
-        multiply("Q", (0, 1), 1, (1,))
-        finish((0, 1), 1)
-        multiply("Q", (0, 1), 2, (0,))
-        multiply("Q", (0, 1), 2, (1,))
-        finish((0, 1), 2)
-        multiply("Q", (0, 1), 3, (0,))
-        multiply("Q", (0, 1), 3, (1,))
-        finish((0, 1), 3)
+        def exact0(t):
+            exact[0, t] = small.tile([P, P], F32, name="exact_top", align_bytes=64)
+            nc.vector.tensor_tensor(
+                out=exact[0, t][:], in0=raw["v", 0, t][:, t:HALF:PACK], in1=raw["w", 0, t][:, t:HALF:PACK], op=MULT
+            )
+
+        def fix0(t):
+            start = t * D + (t // 2) * HALF + t % 2
+            nc.vector.tensor_tensor(
+                out=a_top[:, start : start + RUN - 1 : 2], in0=exact[0, t][:], in1=ident[:], op=ADD
+            )
+
+        def exact1(u):
+            step = HALF + 1
+            band = [
+                raw[name, 1, 1][:, 2 * u * step : (2 * u + 2) * step].rearrange("p (e x) -> p e x", e=2)[:, :, 0:HALF:PACK]
+                for name in "vw"
+            ]
+            exact[1, u] = small.tile([P, 2, P], F32, name="exact_low", align_bytes=64)
+            nc.vector.tensor_tensor(out=exact[1, u][:], in0=band[0], in1=band[1], op=MULT)
+
+        def fix1(u):
+            start = u * (D + 2 * RUN)
+            band = a_low[1][:, start : start + 2 * (RUN + 1)].rearrange("p (e y) -> p e y", e=2)[:, :, 0:RUN:2]
+            nc.vector.tensor_tensor(
+                out=band, in0=exact[1, u][:], in1=ident[:].unsqueeze(1).to_broadcast([P, 2, P]), op=ADD
+            )
+
+        def turn(key, b, source, starts):
+            turned[key] = bank_tile(b)
+            for i, start in enumerate(starts):
+                words = source[:, start : start + RUN].bitcast(F32)
+                nc.tensor.transpose(turned[key][:, i * P : (i + 1) * P], words, ident[:])
+
+        def turn0(t, b):
+            turn(("A", 0, t), b, a_top, [t * D + u * HALF + h * RUN for h in range(2) for u in range(2)])
+
+        def turn1(h, i, b):
+            turn(("A", 1, h, i), b, a_low[h], [(u * PACK + t) * RUN for t in (2 * i, 2 * i + 1) for u in range(2)])
+
+        def turn_p(g, c, i, b):
+            turn(("P", g, c, i), b, rounded[g, c], [(2 * t + u) * RUN for t in (2 * i, 2 * i + 1) for u in range(2)])
+
+        def left0(t, engine):
+            dst = left_top[:].bitcast(F32).rearrange("p (h t r u) -> p h t r u", h=2, t=PACK, u=2)[:, :, t]
+            copy(engine, dst, turned["A", 0, t][:].rearrange("p (h u r) -> p h r u", h=2, u=2))
+
+        def left1(h, i, engine):
+            dst = left_in["A", 1, h].bitcast(F32)[:, i * HALF : (i + 1) * HALF].rearrange("p (t r u) -> p t r u", t=2, u=2)
+            copy(engine, dst, turned["A", 1, h, i][:].rearrange("p (t u r) -> p t r u", t=2, u=2))
+
+        def left_p(g, c, i, engine):
+            dst = left_in["P", g, c].bitcast(F32).rearrange("p (r i x) -> p r i x", i=2, x=PACK)[:, :, i, :]
+            copy(engine, dst, turned["P", g, c, i][:].rearrange("p (x r) -> p r x", x=PACK))
+
+        def right_a(g, c, u, engine):
+            if g == 0:
+                src = a_top[:].rearrange("p (t u h x i) -> p u h x t i", t=PACK, u=2, h=2, i=PACK)[:, u, c]
+            else:
+                src = a_low[c][:, u * D : (u + 1) * D].rearrange("p (t x i) -> p x t i", t=PACK, i=PACK)
+            dst = right_in["A", g, c][:, u * D : (u + 1) * D].rearrange("p (x i t) -> p x t i", t=PACK, i=PACK)
+            copy(engine, dst, src)
+
+        def right_p(g, c, u, engine):
+            src = rounded[g, c][:].rearrange("p (t u a r e) -> p u a t r e", t=PACK, u=2, r=2, e=2)[:, u]
+            dst = right_in["P", g, c][:, u * D : (u + 1) * D].rearrange("p (e a r t) -> p a t r e", t=PACK, r=2, e=2)
+            copy(engine, dst, src)
+
+        def quantize(source, planes, first, count):
+            words = slice(first * RUN, (first + count) * RUN)
+            nc.vector.quantize_mx(
+                out=planes[0][:, words].bitcast(FP8X4),
+                scales=planes[1][:, words],
+                in_=source[:, first * D : (first + count) * D],
+            )
+
+        def q_left_a(g, h):
+            quantize(left_in["A", g, h], left["A", g, h], 0, 2)
+
+        def q_right_a(g, c):
+            quantize(right_in["A", g, c], right["A", g, c], 0, 2)
+
+        def q_left_p(g, c):
+            quantize(left_in["P", g, c], left["P", g, c], 0, 2)
+
+        def q_right_p(g, c, us):
+            quantize(right_in["P", g, c], right["P", g, c], us[0], len(us))
+
+        def multiply(key, b, fixed, t, moving):
+            first = key not in sums
+            if first:
+                sums[key] = bank_tile(b)
+            cols = slice(t * P, (t + 1) * P)
+            nc.tensor.matmul_mx(
+                out=sums[key][:],
+                lhsT=fixed[0][:, cols].bitcast(FP8X4),
+                lhsT_scale=fixed[1][:, cols],
+                rhs=moving[0][:].bitcast(FP8X4),
+                rhs_scale=moving[1][:],
+                start=first,
+                stop=not first,
+            )
+
+        def square(g, c, t, h, b=None):
+            multiply(("P", g, c, t), b, left["A", g, h], t, right["A", h, c])
+
+        def fourth(g, j, t, h, b=None):
+            multiply(("Q", g, j, t), b, right["P", h, g], t, left["P", j, h])
+
+        def round_p(g, c, t, engine):
+            copy(engine, rounded[g, c][:, t * HALF : (t + 1) * HALF], sums["P", g, c, t][:])
+
+        def finish(g, j, t):
+            if g == 0:
+                factor = raw["w", 0, t][:, j * HALF : (j + 1) * HALF]
+            else:
+                factor = raw["w", 1, j][:, t * HALF : (t + 1) * HALF]
+            result = outs.tile([P, HALF], F32, name="result")
+            nc.vector.tensor_tensor(out=result[:], in0=sums["Q", g, j, t][:], in1=factor, op=MULT)
+            nc.sync.dma_start(out=rows(out, g)[:, t, j * HALF : (j + 1) * HALF], in_=result[:])
+
+        for t in range(4):
+            load0(t)
+        load1(0)
+        load1(1)
+        for t in range(4):
+            product0(t)
+            exact0(t)
+            fix0(t)
+            turn0(t,4+t)
+            if t<3:
+                left0(t,"S")
+        right_a(0,0,0,"S")
+        right_a(0,0,1,"V")
+        left0(3,"S")
+        product1(0,0)
+        product1(0,1)
+        right_a(1,0,0,"S")
+        q_right_a(0,0)
+        q_left_a(0,0)
+        right_a(1,0,1,"V")
+        q_left_a(0,1)
+        q_right_a(1,0)
+        turn1(0,0,4)
+        turn1(0,1,5)
+        for t in range(4):
+            square(0,0,t,0,t)
+        for t in range(4):
+            square(0,0,t,1)
+        right_a(0,1,0,"S")
+        left1(0,0,"S")
+        left1(0,1,"S")
+        right_a(0,1,1,"S")
+        product1(1,0)
+        exact1(0)
+        product1(1,1)
+        fix1(0)
+        exact1(1)
+        q_right_a(0,1)
+        fix1(1)
+        right_a(1,1,0,"V")
+        right_a(1,1,1,"V")
+        q_left_a(1,0)
+        q_right_a(1,1)
+        for t in range(4):
+            round_p(0,0,t,"S")
+        for t in range(4):
+            square(0,1,t,0,4+t)
+        turn1(1,0,0)
+        turn1(1,1,1)
+        turn_p(0,0,0,2)
+        turn_p(0,0,1,3)
+        left1(1,0,"S")
+        left1(1,1,"S")
+        left_p(0,0,0,"S")
+        left_p(0,0,1,"S")
+        for t in range(4):
+            square(0,1,t,1)
+        right_p(0,0,0,"V")
+        q_left_a(1,1)
+        right_p(0,0,1,"V")
+        for t in range(4):
+            square(1,0,t,0,t)
+            square(1,0,t,1)
+        for t in range(4):
+            round_p(0,1,t,"VSSS"[t])
+        q_right_p(0,0,[0,1])
+        q_left_p(0,0)
+        turn_p(0,1,0,4)
+        turn_p(0,1,1,5)
+        for t in range(4):
+            round_p(1,0,t,"VSVS"[t])
+        left_p(0,1,0,"S")
+        left_p(0,1,1,"S")
+        for t in range(4):
+            square(1,1,t,0,(6,7,0,1)[t])
+            square(1,1,t,1)
+        right_p(1,0,0,"V")
+        right_p(1,0,1,"V")
+        q_right_p(1,0,[0])
+        q_left_p(0,1)
+        q_right_p(1,0,[1])
+        for t in range(4):
+            round_p(1,1,t,"S")
+        for t in range(2):
+            fourth(0,0,t,0,4+t)
+            fourth(0,0,t,1)
+        turn_p(1,0,0,2)
+        turn_p(1,0,1,3)
+        turn_p(1,1,0,6)
+        turn_p(1,1,1,7)
+        for t in range(2,4):
+            fourth(0,0,t,0,t-2)
+            fourth(0,0,t,1)
+        for i in (0,1):
+            left_p(1,0,i,"S")
+        for i in (0,1):
+            left_p(1,1,i,"S")
+        finish(0,0,0)
+        finish(0,0,1)
+        right_p(0,1,0,"V")
+        q_left_p(1,0)
+        finish(0,0,2)
+        q_left_p(1,1)
+        finish(0,0,3)
+        right_p(1,1,0,"S")
+        right_p(0,1,1,"S")
+        right_p(1,1,1,"S")
+        for t in range(4):
+            fourth(0,1,t,0,4+t)
+            fourth(0,1,t,1)
+        q_right_p(0,1,[0])
+        finish(0,1,0)
+        q_right_p(1,1,[0])
+        finish(0,1,1)
+        finish(0,1,2)
+        q_right_p(0,1,[1])
+        finish(0,1,3)
+        for t in range(2):
+            for j in (0,1):
+                fourth(1,j,t,0,2*t+j)
+                fourth(1,j,t,1)
+        q_right_p(1,1,[1])
+        finish(1,0,0)
+        finish(1,1,0)
+        finish(1,0,1)
+        finish(1,1,1)
+        for t in range(2,4):
+            for j in (0,1):
+                fourth(1,j,t,0,2*t+j)
+                fourth(1,j,t,1)
+                finish(1,j,t)

@@ -42,7 +42,11 @@ def tile_notears_acyclicity_gradient_s7_kernel(tc, w, v, out):
         a_top = values("a_top", 2 * QUAD)
         a_low = [values("a_low%d" % h, QUAD + PAD) for h in range(2)]
         left_top = values("left_top", 2 * QUAD)
-        left_in = {("A", 0, h): left_top[:, h * QUAD : (h + 1) * QUAD] for h in range(2)}
+        left_in = {}
+        top_planes = (
+            keep.tile([P, D], U32, name="codes_top", align_bytes=64),
+            keep.tile([P, D], U8, name="scales_top", align_bytes=64),
+        )
         for m, g, h in [("A", 1, 0), ("A", 1, 1)] + [("P", g, h) for g, h in quads]:
             left_in[m, g, h] = values("left_in%s%d%d" % (m, g, h), QUAD)[:]
         right_in = {(m, g, h): values("right_in%s%d%d" % (m, g, h), QUAD)[:] for m in "AP" for g, h in quads}
@@ -50,6 +54,8 @@ def tile_notears_acyclicity_gradient_s7_kernel(tc, w, v, out):
         for side, planes in (("left", left), ("right", right)):
             for m in "AP":
                 for g, h in quads:
+                    if (side, m, g) == ("left", "A", 0):
+                        continue
                     name = "%s%s%d%d" % (side, m, g, h)
                     codes = keep.tile([P, HALF], U32, name="codes_" + name, align_bytes=64)
                     scales = keep.tile([P, HALF], U8, name="scales_" + name, align_bytes=64)
@@ -140,7 +146,7 @@ def tile_notears_acyclicity_gradient_s7_kernel(tc, w, v, out):
             turn(("P", g, c, i), b, rounded[g, c], [(2 * t + u) * RUN for t in (2 * i, 2 * i + 1) for u in range(2)])
 
         def left0(t, engine):
-            dst = left_top[:].bitcast(F32).rearrange("p (h t r u) -> p h t r u", h=2, t=PACK, u=2)[:, :, t]
+            dst = left_top[:, t * D : (t + 1) * D].bitcast(F32).rearrange("p (h r u) -> p h r u", h=2, u=2)
             copy(engine, dst, turned["A", 0, t][:].rearrange("p (h u r) -> p h r u", h=2, u=2))
 
         def left1(h, i, engine):
@@ -172,6 +178,9 @@ def tile_notears_acyclicity_gradient_s7_kernel(tc, w, v, out):
                 in_=source[:, first * D : (first + count) * D],
             )
 
+        def q_left0(t):
+            quantize(left_top, top_planes, t, 1)
+
         def q_left_a(g, h):
             quantize(left_in["A", g, h], left["A", g, h], 0, 2)
 
@@ -200,7 +209,10 @@ def tile_notears_acyclicity_gradient_s7_kernel(tc, w, v, out):
             )
 
         def square(g, c, t, h, b=None):
-            multiply(("P", g, c, t), b, left["A", g, h], t, right["A", h, c])
+            if g == 0:
+                multiply(("P", g, c, t), b, top_planes, 2 * t + h, right["A", h, c])
+            else:
+                multiply(("P", g, c, t), b, left["A", g, h], t, right["A", h, c])
 
         def fourth(g, j, t, h, b=None):
             multiply(("Q", g, j, t), b, right["P", h, g], t, left["P", j, h])
@@ -224,6 +236,8 @@ def tile_notears_acyclicity_gradient_s7_kernel(tc, w, v, out):
         for t in range(4):
             product0(t)
             exact0(t)
+            if t>=2:
+                q_left0(t-2)
             fix0(t)
             turn0(t,4+t)
             if t<3:
@@ -231,25 +245,27 @@ def tile_notears_acyclicity_gradient_s7_kernel(tc, w, v, out):
         right_a(0,0,0,"S")
         right_a(0,0,1,"V")
         left0(3,"S")
+        q_left0(2)
         product1(0,0)
-        product1(0,1)
         right_a(1,0,0,"S")
         q_right_a(0,0)
-        q_left_a(0,0)
+        product1(0,1)
+        q_left0(3)
         right_a(1,0,1,"V")
-        q_left_a(0,1)
+        product1(1,0)
         q_right_a(1,0)
-        turn1(0,0,4)
-        turn1(0,1,5)
         for t in range(4):
             square(0,0,t,0,t)
         for t in range(4):
             square(0,0,t,1)
+        turn1(0,0,4)
+        turn1(0,1,5)
         right_a(0,1,0,"S")
+        right_a(0,1,1,"S")
+        for t in range(4):
+            round_p(0,0,t,"S")
         left1(0,0,"S")
         left1(0,1,"S")
-        right_a(0,1,1,"S")
-        product1(1,0)
         exact1(0)
         product1(1,1)
         fix1(0)
@@ -258,93 +274,84 @@ def tile_notears_acyclicity_gradient_s7_kernel(tc, w, v, out):
         fix1(1)
         right_a(1,1,0,"V")
         right_a(1,1,1,"V")
-        q_left_a(1,0)
+        right_p(0,0,0,"V")
         q_right_a(1,1)
-        for t in range(4):
-            round_p(0,0,t,"S")
-        for t in range(4):
-            square(0,1,t,0,4+t)
-        turn1(1,0,0)
-        turn1(1,1,1)
-        turn_p(0,0,0,2)
-        turn_p(0,0,1,3)
+        q_left_a(1,0)
+        for t in range(2):
+            square(0,1,t,0,6+t)
+        turn1(1,0,2)
+        turn1(1,1,3)
+        for t in range(2,4):
+            square(0,1,t,0,t-2)
+        turn_p(0,0,0,4)
+        turn_p(0,0,1,5)
         left1(1,0,"S")
         left1(1,1,"S")
         left_p(0,0,0,"S")
         left_p(0,0,1,"S")
         for t in range(4):
             square(0,1,t,1)
-        right_p(0,0,0,"V")
         q_left_a(1,1)
         right_p(0,0,1,"V")
         for t in range(4):
-            square(1,0,t,0,t)
+            square(1,0,t,0,2+t)
             square(1,0,t,1)
         for t in range(4):
             round_p(0,1,t,"VSSS"[t])
         q_right_p(0,0,[0,1])
         q_left_p(0,0)
-        turn_p(0,1,0,4)
-        turn_p(0,1,1,5)
+        turn_p(0,1,0,6)
+        turn_p(0,1,1,7)
         for t in range(4):
-            round_p(1,0,t,"VSVS"[t])
+            round_p(1,0,t,"SSVS"[t])
         left_p(0,1,0,"S")
         left_p(0,1,1,"S")
         for t in range(4):
-            square(1,1,t,0,(6,7,0,1)[t])
+            square(1,1,t,0,t)
             square(1,1,t,1)
+        right_p(0,1,0,"V")
         right_p(1,0,0,"V")
         right_p(1,0,1,"V")
         q_right_p(1,0,[0])
         q_left_p(0,1)
         q_right_p(1,0,[1])
+        q_right_p(0,1,[0])
         for t in range(4):
             round_p(1,1,t,"S")
         for t in range(2):
             fourth(0,0,t,0,4+t)
             fourth(0,0,t,1)
-        turn_p(1,0,0,2)
-        turn_p(1,0,1,3)
-        turn_p(1,1,0,6)
-        turn_p(1,1,1,7)
+        turn_p(1,0,0,6)
+        turn_p(1,0,1,7)
         for t in range(2,4):
             fourth(0,0,t,0,t-2)
             fourth(0,0,t,1)
-        for i in (0,1):
-            left_p(1,0,i,"S")
-        for i in (0,1):
-            left_p(1,1,i,"S")
+        turn_p(1,1,0,2)
+        turn_p(1,1,1,3)
+        right_p(1,1,0,"S")
+        left_p(1,0,0,"S")
+        left_p(1,0,1,"S")
+        right_p(1,1,1,"S")
+        left_p(1,1,0,"S")
+        left_p(1,1,1,"S")
         finish(0,0,0)
         finish(0,0,1)
-        right_p(0,1,0,"V")
-        q_left_p(1,0)
-        finish(0,0,2)
-        q_left_p(1,1)
-        finish(0,0,3)
-        right_p(1,1,0,"S")
-        right_p(0,1,1,"S")
-        right_p(1,1,1,"S")
-        for t in range(4):
-            fourth(0,1,t,0,4+t)
-            fourth(0,1,t,1)
-        q_right_p(0,1,[0])
-        finish(0,1,0)
+        right_p(0,1,1,"V")
         q_right_p(1,1,[0])
-        finish(0,1,1)
-        finish(0,1,2)
+        finish(0,0,2)
         q_right_p(0,1,[1])
-        finish(0,1,3)
-        for t in range(2):
-            for j in (0,1):
-                fourth(1,j,t,0,2*t+j)
-                fourth(1,j,t,1)
+        finish(0,0,3)
+        q_left_p(1,0)
         q_right_p(1,1,[1])
+        for t in range(4):
+            fourth(1,0,t,0,4+t)
+            fourth(1,0,t,1)
         finish(1,0,0)
-        finish(1,1,0)
-        finish(1,0,1)
-        finish(1,1,1)
-        for t in range(2,4):
-            for j in (0,1):
-                fourth(1,j,t,0,2*t+j)
-                fourth(1,j,t,1)
-                finish(1,j,t)
+        q_left_p(1,1)
+        for t in range(1,4):
+            finish(1,0,t)
+        for g in (0,1):
+            for t in range(4):
+                fourth(g,1,t,0,4*g+t)
+                fourth(g,1,t,1)
+                finish(g,1,t)

@@ -32,7 +32,6 @@ def tile_notears_acyclicity_gradient_s7_kernel(tc, w, v, out):
         ctx.enter_context(tc.manual_schedule())
 
         ident = keep.tile([P, P], F32, name="ident", align_bytes=64)
-        make_identity(nc, ident[:])
 
         def values(name, width):
             return keep.tile([P, width], BF16, name=name, align_bytes=64)
@@ -73,10 +72,13 @@ def tile_notears_acyclicity_gradient_s7_kernel(tc, w, v, out):
         def rows(x, g):
             return x[g * HALF : (g + 1) * HALF, :].rearrange("(p t) j -> p t j", t=PACK)
 
+        def identity():
+            make_identity(nc, ident[:])
+
         def load0(t):
-            for name, x in (("v", v), ("w", w)):
+            for name, x, queue in (("v", v, nc.sync), ("w", w, nc.scalar)):
                 raw[name, 0, t] = values("%s_top%d" % (name, t), D)
-                nc.sync.dma_start(out=raw[name, 0, t][:], in_=rows(x, 0)[:, t, :])
+                queue.dma_start(out=raw[name, 0, t][:], in_=rows(x, 0)[:, t, :])
 
         def load1(h):
             for name, x in (("v", v), ("w", w)):
@@ -227,12 +229,14 @@ def tile_notears_acyclicity_gradient_s7_kernel(tc, w, v, out):
                 factor = raw["w", 1, j][:, t * HALF : (t + 1) * HALF]
             result = outs.tile([P, HALF], F32, name="result")
             nc.vector.tensor_tensor(out=result[:], in0=sums["Q", g, j, t][:], in1=factor, op=MULT)
-            nc.sync.dma_start(out=rows(out, g)[:, t, j * HALF : (j + 1) * HALF], in_=result[:])
+            queue = nc.scalar if j == 1 and t % 2 == 1 else nc.sync
+            queue.dma_start(out=rows(out, g)[:, t, j * HALF : (j + 1) * HALF], in_=result[:])
 
         for t in range(4):
             load0(t)
         load1(0)
         load1(1)
+        identity()
         for t in range(4):
             product0(t)
             exact0(t)
@@ -347,11 +351,21 @@ def tile_notears_acyclicity_gradient_s7_kernel(tc, w, v, out):
             fourth(1,0,t,0,4+t)
             fourth(1,0,t,1)
         finish(1,0,0)
+        finish(1,0,1)
         q_left_p(1,1)
-        for t in range(1,4):
-            finish(1,0,t)
-        for g in (0,1):
-            for t in range(4):
-                fourth(g,1,t,0,4*g+t)
-                fourth(g,1,t,1)
-                finish(g,1,t)
+        finish(1,0,2)
+        finish(1,0,3)
+        for t in range(2):
+            fourth(0,1,t,0,t)
+        for t in range(2):
+            fourth(0,1,t,1)
+        for t in range(2):
+            finish(0,1,t)
+        for t in range(2,4):
+            fourth(0,1,t,0,t)
+            fourth(0,1,t,1)
+            finish(0,1,t)
+        for t in range(4):
+            fourth(1,1,t,0,4+t)
+            fourth(1,1,t,1)
+            finish(1,1,t)

from contextlib import ExitStack

import concourse.mybir as mybir
from concourse.masks import make_identity

D = 1024
FLOPS = 2 * 2 * D * D * D

F32 = mybir.dt.float32
BF16 = mybir.dt.bfloat16
U32 = mybir.dt.uint32
U8 = mybir.dt.uint8
FP8X4 = mybir.dt.float8_e4m3fn_x4
MULT = mybir.AluOpType.mult
ADD = mybir.AluOpType.add

P = 128
PACK = 4
HALF = P * PACK
QUAD = PACK * HALF
RUN = 2 * P
PAD = 32


def tile_notears_acyclicity_gradient_s7_kernel(tc, w, v, out):
    nc = tc.nc
    with ExitStack() as ctx:
        keep = ctx.enter_context(tc.tile_pool(name="keep", bufs=1))
        small = ctx.enter_context(tc.tile_pool(name="small", bufs=2))
        outs = ctx.enter_context(tc.tile_pool(name="outs", bufs=8))
        psum = ctx.enter_context(tc.psum_pool(name="psum", bufs=1))
        ctx.enter_context(tc.manual_schedule())

        ident = keep.tile([P, P], F32, name="ident", align_bytes=64)

        def values(name, width):
            return keep.tile([P, width], BF16, name=name, align_bytes=64)

        quads = [(g, h) for g in range(2) for h in range(2)]
        raw, exact, turned, sums, left, right = {}, {}, {}, {}, {}, {}
        a_top = values("a_top", 2 * QUAD)
        a_low = [values("a_low%d" % h, QUAD + PAD) for h in range(2)]
        left_top = values("left_top", 2 * QUAD)
        left_in = {}
        top_planes = (
            keep.tile([P, D], U32, name="codes_top", align_bytes=64),
            keep.tile([P, D], U8, name="scales_top", align_bytes=64),
        )
        for m, g, h in [("A", 1, 0), ("A", 1, 1)] + [("P", g, h) for g, h in quads]:
            left_in[m, g, h] = values("left_in%s%d%d" % (m, g, h), QUAD)[:]
        right_in = {(m, g, h): values("right_in%s%d%d" % (m, g, h), QUAD)[:] for m in "AP" for g, h in quads}
        rounded = {q: values("rounded%d%d" % q, QUAD) for q in quads}
        for side, planes in (("left", left), ("right", right)):
            for m in "AP":
                for g, h in quads:
                    if (side, m, g) == ("left", "A", 0):
                        continue
                    name = "%s%s%d%d" % (side, m, g, h)
                    codes = keep.tile([P, HALF], U32, name="codes_" + name, align_bytes=64)
                    scales = keep.tile([P, HALF], U8, name="scales_" + name, align_bytes=64)
                    planes[m, g, h] = (codes, scales)

        def bank_tile(b):
            return psum.tile([P, HALF], F32, name="bank%d" % b, tag="bank%d" % b)

        def copy(engine, dst, src):
            if engine == "S":
                nc.scalar.copy(out=dst, in_=src)
            else:
                nc.vector.tensor_copy(out=dst, in_=src)

        def rows(x, g):
            return x[g * HALF : (g + 1) * HALF, :].rearrange("(p t) j -> p t j", t=PACK)

        def identity():
            make_identity(nc, ident[:])

        def load0(t):
            for name, x, queue in (("v", v, nc.sync), ("w", w, nc.scalar)):
                raw[name, 0, t] = values("%s_top%d" % (name, t), D)
                queue.dma_start(out=raw[name, 0, t][:], in_=rows(x, 0)[:, t, :])

        def load1(h):
            for name, x in (("v", v), ("w", w)):
                raw[name, 1, h] = values("%s_low%d" % (name, h), QUAD + PAD)
                nc.sync.dma_start(
                    out=raw[name, 1, h][:, 0:QUAD].rearrange("p (t j) -> p t j", t=PACK),
                    in_=rows(x, 1)[:, :, h * HALF : (h + 1) * HALF],
                )

        def product0(t):
            nc.vector.tensor_tensor(
                out=a_top[:, t * D : (t + 1) * D].rearrange("p (u x e) -> p u x e", u=2, e=2),
                in0=raw["v", 0, t][:].rearrange("p (x u e) -> p u x e", u=2, e=2),
                in1=raw["w", 0, t][:].rearrange("p (x u e) -> p u x e", u=2, e=2),
                op=MULT,
            )

        def product1(h, u):
            nc.vector.tensor_tensor(
                out=a_low[h][:, u * D : (u + 1) * D].rearrange("p (x e) -> p x e", e=2),
                in0=raw["v", 1, h][:, 0:QUAD].rearrange("p (x u e) -> p x u e", u=2, e=2)[:, :, u, :],
                in1=raw["w", 1, h][:, 0:QUAD].rearrange("p (x u e) -> p x u e", u=2, e=2)[:, :, u, :],
                op=MULT,
            )

        def exact0(t):
            exact[0, t] = small.tile([P, P], F32, name="exact_top", align_bytes=64)
            nc.vector.tensor_tensor(
                out=exact[0, t][:], in0=raw["v", 0, t][:, t:HALF:PACK], in1=raw["w", 0, t][:, t:HALF:PACK], op=MULT
            )

        def fix0(t):
            start = t * D + (t // 2) * HALF + t % 2
            nc.vector.tensor_tensor(
                out=a_top[:, start : start + RUN - 1 : 2], in0=exact[0, t][:], in1=ident[:], op=ADD
            )

        def exact1(u):
            step = HALF + 1
            band = [
                raw[name, 1, 1][:, 2 * u * step : (2 * u + 2) * step].rearrange("p (e x) -> p e x", e=2)[:, :, 0:HALF:PACK]
                for name in "vw"
            ]
            exact[1, u] = small.tile([P, 2, P], F32, name="exact_low", align_bytes=64)
            nc.vector.tensor_tensor(out=exact[1, u][:], in0=band[0], in1=band[1], op=MULT)

        def fix1(u):
            start = u * (D + 2 * RUN)
            band = a_low[1][:, start : start + 2 * (RUN + 1)].rearrange("p (e y) -> p e y", e=2)[:, :, 0:RUN:2]
            nc.vector.tensor_tensor(
                out=band, in0=exact[1, u][:], in1=ident[:].unsqueeze(1).to_broadcast([P, 2, P]), op=ADD
            )

        def turn(key, b, source, starts):
            turned[key] = bank_tile(b)
            for i, start in enumerate(starts):
                words = source[:, start : start + RUN].bitcast(F32)
                nc.tensor.transpose(turned[key][:, i * P : (i + 1) * P], words, ident[:])

        def turn0(t, b):
            turn(("A", 0, t), b, a_top, [t * D + u * HALF + h * RUN for h in range(2) for u in range(2)])

        def turn1(h, i, b):
            turn(("A", 1, h, i), b, a_low[h], [(u * PACK + t) * RUN for t in (2 * i, 2 * i + 1) for u in range(2)])

        def turn_p(g, c, i, b):
            turn(("P", g, c, i), b, rounded[g, c], [(2 * t + u) * RUN for t in (2 * i, 2 * i + 1) for u in range(2)])

        def left0(t, engine):
            dst = left_top[:, t * D : (t + 1) * D].bitcast(F32).rearrange("p (h r u) -> p h r u", h=2, u=2)
            copy(engine, dst, turned["A", 0, t][:].rearrange("p (h u r) -> p h r u", h=2, u=2))

        def left1(h, i, engine):
            dst = left_in["A", 1, h].bitcast(F32)[:, i * HALF : (i + 1) * HALF].rearrange("p (t r u) -> p t r u", t=2, u=2)
            copy(engine, dst, turned["A", 1, h, i][:].rearrange("p (t u r) -> p t r u", t=2, u=2))

        def left_p(g, c, i, engine):
            dst = left_in["P", g, c].bitcast(F32).rearrange("p (r i x) -> p r i x", i=2, x=PACK)[:, :, i, :]
            copy(engine, dst, turned["P", g, c, i][:].rearrange("p (x r) -> p r x", x=PACK))

        def right_a(g, c, u, engine):
            if g == 0:
                src = a_top[:].rearrange("p (t u h x i) -> p u h x t i", t=PACK, u=2, h=2, i=PACK)[:, u, c]
            else:
                src = a_low[c][:, u * D : (u + 1) * D].rearrange("p (t x i) -> p x t i", t=PACK, i=PACK)
            dst = right_in["A", g, c][:, u * D : (u + 1) * D].rearrange("p (x i t) -> p x t i", t=PACK, i=PACK)
            copy(engine, dst, src)

        def right_p(g, c, u, engine):
            src = rounded[g, c][:].rearrange("p (t u a r e) -> p u a t r e", t=PACK, u=2, r=2, e=2)[:, u]
            dst = right_in["P", g, c][:, u * D : (u + 1) * D].rearrange("p (e a r t) -> p a t r e", t=PACK, r=2, e=2)
            copy(engine, dst, src)

        def quantize(source, planes, first, count):
            words = slice(first * RUN, (first + count) * RUN)
            nc.vector.quantize_mx(
                out=planes[0][:, words].bitcast(FP8X4),
                scales=planes[1][:, words],
                in_=source[:, first * D : (first + count) * D],
            )

        def q_left0(t):
            quantize(left_top, top_planes, t, 1)

        def q_left_a(g, h):
            quantize(left_in["A", g, h], left["A", g, h], 0, 2)

        def q_right_a(g, c):
            quantize(right_in["A", g, c], right["A", g, c], 0, 2)

        def q_left_p(g, c):
            quantize(left_in["P", g, c], left["P", g, c], 0, 2)

        def q_right_p(g, c, us):
            quantize(right_in["P", g, c], right["P", g, c], us[0], len(us))

        def multiply(key, b, fixed, t, moving):
            first = key not in sums
            if first:
                sums[key] = bank_tile(b)
            cols = slice(t * P, (t + 1) * P)
            nc.tensor.matmul_mx(
                out=sums[key][:],
                lhsT=fixed[0][:, cols].bitcast(FP8X4),
                lhsT_scale=fixed[1][:, cols],
                rhs=moving[0][:].bitcast(FP8X4),
                rhs_scale=moving[1][:],
                start=first,
                stop=not first,
            )

        def square(g, c, t, h, b=None):
            if g == 0:
                multiply(("P", g, c, t), b, top_planes, 2 * t + h, right["A", h, c])
            else:
                multiply(("P", g, c, t), b, left["A", g, h], t, right["A", h, c])

        def fourth(g, j, t, h, b=None):
            multiply(("Q", g, j, t), b, right["P", h, g], t, left["P", j, h])

        def round_p(g, c, t, engine):
            copy(engine, rounded[g, c][:, t * HALF : (t + 1) * HALF], sums["P", g, c, t][:])

        def finish(g, j, t):
            if g == 0:
                factor = raw["w", 0, t][:, j * HALF : (j + 1) * HALF]
            else:
                factor = raw["w", 1, j][:, t * HALF : (t + 1) * HALF]
            result = outs.tile([P, HALF], F32, name="result")
            nc.vector.tensor_tensor(out=result[:], in0=sums["Q", g, j, t][:], in1=factor, op=MULT)
            queue = nc.scalar if j == 1 and t % 2 == 1 else nc.sync
            queue.dma_start(out=rows(out, g)[:, t, j * HALF : (j + 1) * HALF], in_=result[:])

        for t in range(4):
            load0(t)
        load1(0)
        load1(1)
        identity()
        for t in range(4):
            product0(t)
            exact0(t)
            if t>=2:
                q_left0(t-2)
            fix0(t)
            turn0(t,4+t)
            if t<3:
                left0(t,"S")
        right_a(0,0,0,"S")
        right_a(0,0,1,"V")
        left0(3,"S")
        q_left0(2)
        product1(0,0)
        right_a(1,0,0,"S")
        q_right_a(0,0)
        product1(0,1)
        q_left0(3)
        right_a(1,0,1,"V")
        product1(1,0)
        q_right_a(1,0)
        for t in range(4):
            square(0,0,t,0,t)
        for t in range(4):
            square(0,0,t,1)
        turn1(0,0,4)
        turn1(0,1,5)
        right_a(0,1,0,"S")
        right_a(0,1,1,"S")
        for t in range(4):
            round_p(0,0,t,"S")
        left1(0,0,"S")
        left1(0,1,"S")
        exact1(0)
        product1(1,1)
        fix1(0)
        exact1(1)
        q_right_a(0,1)
        fix1(1)
        right_a(1,1,0,"V")
        right_a(1,1,1,"V")
        right_p(0,0,0,"V")
        q_right_a(1,1)
        q_left_a(1,0)
        for t in range(2):
            square(0,1,t,0,6+t)
        turn1(1,0,2)
        turn1(1,1,3)
        for t in range(2,4):
            square(0,1,t,0,t-2)
        turn_p(0,0,0,4)
        turn_p(0,0,1,5)
        left1(1,0,"S")
        left1(1,1,"S")
        left_p(0,0,0,"S")
        left_p(0,0,1,"S")
        for t in range(4):
            square(0,1,t,1)
        q_left_a(1,1)
        right_p(0,0,1,"V")
        for t in range(4):
            square(1,0,t,0,2+t)
            square(1,0,t,1)
        for t in range(4):
            round_p(0,1,t,"VSSS"[t])
        q_right_p(0,0,[0,1])
        q_left_p(0,0)
        turn_p(0,1,0,6)
        turn_p(0,1,1,7)
        for t in range(4):
            round_p(1,0,t,"SSVS"[t])
        left_p(0,1,0,"S")
        left_p(0,1,1,"S")
        for t in range(4):
            square(1,1,t,0,t)
            square(1,1,t,1)
        right_p(0,1,0,"V")
        right_p(1,0,0,"V")
        right_p(1,0,1,"V")
        q_right_p(1,0,[0])
        q_left_p(0,1)
        q_right_p(1,0,[1])
        q_right_p(0,1,[0])
        for t in range(4):
            round_p(1,1,t,"S")
        for t in range(2):
            fourth(0,0,t,0,4+t)
            fourth(0,0,t,1)
        turn_p(1,0,0,6)
        turn_p(1,0,1,7)
        for t in range(2,4):
            fourth(0,0,t,0,t-2)
            fourth(0,0,t,1)
        turn_p(1,1,0,2)
        turn_p(1,1,1,3)
        right_p(1,1,0,"S")
        left_p(1,0,0,"S")
        left_p(1,0,1,"S")
        right_p(1,1,1,"S")
        left_p(1,1,0,"S")
        left_p(1,1,1,"S")
        finish(0,0,0)
        finish(0,0,1)
        right_p(0,1,1,"V")
        q_right_p(1,1,[0])
        finish(0,0,2)
        q_right_p(0,1,[1])
        finish(0,0,3)
        q_left_p(1,0)
        q_right_p(1,1,[1])
        for t in range(4):
            fourth(1,0,t,0,4+t)
            fourth(1,0,t,1)
        finish(1,0,0)
        finish(1,0,1)
        q_left_p(1,1)
        finish(1,0,2)
        finish(1,0,3)
        for t in range(2):
            fourth(0,1,t,0,t)
        for t in range(2):
            fourth(0,1,t,1)
        for t in range(2):
            finish(0,1,t)
        for t in range(2,4):
            fourth(0,1,t,0,t)
            fourth(0,1,t,1)
            finish(0,1,t)
        for t in range(4):
            fourth(1,1,t,0,4+t)
            fourth(1,1,t,1)
            finish(1,1,t)
